import numpy as np
import ml_dtypes


def mxq(x, axis, fmt="e4m3"):
    dtype, down = {"e4m3": (ml_dtypes.float8_e4m3fn, 7), "e5m2": (ml_dtypes.float8_e5m2, 14)}[fmt]
    v = np.moveaxis(np.asarray(x, np.float32).astype(ml_dtypes.bfloat16).astype(np.float64), axis, -1)
    blocks = v.reshape(v.shape[:-1] + (-1, 32))
    amax = np.abs(blocks).max(-1, keepdims=True)
    byte = np.maximum(np.where(amax > 0, np.frexp(amax)[1] - 1 + 127, 0) - down, 1)
    scale = np.exp2(byte - 127.0)
    codes = (blocks / scale).astype(np.float32).astype(dtype).astype(np.float64)
    return np.moveaxis((codes * scale).reshape(v.shape), -1, axis)


WIDE = False


def mx_kscale(k):
    if not WIDE:
        return np.ones(k)
    levels = np.array([30, -30])
    if k % 512:
        return np.exp2(np.random.permutation(np.resize(levels, k // 32))).repeat(32)
    a = np.empty((k // 512, 16))
    for p in range(k // 512):
        a[p, :8] = np.random.permutation(np.resize(levels, 8))
        for g in range(8):
            far = levels[np.abs(levels - a[p, g]) >= 10]
            a[p, g + 8] = far[np.random.randint(len(far))]
    return np.exp2(a.ravel()).repeat(32)


def f64(x):
    return np.asarray(x).astype(np.float64)


def striped(idx):
    return np.tile(np.asarray(idx).reshape(-1, 16).T, (8, 1)).astype(np.uint16)


def unstriped(offs):
    return offs[:16].T.reshape(-1).astype(np.int64)


E2M1 = np.array([0.0, 0.5, 1.0, 1.5, 2.0, 3.0, 4.0, 6.0, -0.0, -0.5, -1.0, -1.5, -2.0, -3.0, -4.0, -6.0])


def pack_weight(w, fmt):
    k, n = w.shape
    w = f64(np.asarray(w, np.float32).astype(ml_dtypes.bfloat16)).reshape(k // 32, 32, n)
    amax = np.abs(w).max(1)
    if fmt in ("e4m3", "e5m2"):
        byte = np.frexp(amax)[1] - 1 + 127 - (7 if fmt == "e4m3" else 14)
    else:
        mant, ex = np.frexp(amax / 6.0)
        byte = np.where(mant > 0.5, ex, ex - 1) + 127
    byte = np.clip(np.where(amax > 0, byte, 1), 1, 254)
    scaled = (w * np.exp2(127.0 - byte)[:, None, :]).reshape(k, n).astype(np.float32)
    by_word = np.ascontiguousarray(scaled.reshape(k // 512, 128, 4, n).transpose(0, 1, 3, 2))
    if fmt in ("e4m3", "e5m2"):
        words = by_word.astype(ml_dtypes.float8_e4m3fn if fmt == "e4m3" else ml_dtypes.float8_e5m2).view(np.uint8)
    else:
        c = by_word.astype(ml_dtypes.float4_e2m1fn).view(np.uint8) & 0xF
        words = (c[..., 0::2] | (c[..., 1::2] << 4)).reshape(k // 512, 128, 2 * n)
    return np.ascontiguousarray(words), np.ascontiguousarray(byte.astype(np.uint8).reshape(k // 512, 16, n))


def unpack_weight(words, scales, fmt):
    g, _, n = scales.shape
    words = np.ascontiguousarray(words).reshape(g, 128, n, -1)
    if fmt in ("e4m3", "e5m2"):
        vals = words.view(ml_dtypes.float8_e4m3fn if fmt == "e4m3" else ml_dtypes.float8_e5m2).astype(np.float64)
    else:
        nib = np.empty((g, 128, n, 4), np.uint8)
        nib[..., 0::2] = words & 0xF
        nib[..., 1::2] = words >> 4
        vals = E2M1[nib]
    vals = vals * np.repeat(np.exp2(scales.astype(np.float64) - 127.0), 8, axis=1)[..., None]
    return vals.transpose(0, 1, 3, 2).reshape(g * 512, n)


K, T, J, R, F, Z, N = 512, 512, 256, 512, 512, 1024, 256


def setup_inputs():
    n = np.random.standard_normal
    idx = np.random.permutation(T)[:J]
    idx2 = np.random.permutation(Z)[:J]
    fk = mx_kscale(K)
    fr = mx_kscale(R)
    ff = mx_kscale(F)
    wp = pack_weight(n((K, R)) * 1 / np.sqrt(K) * fk[:, None] * fr, "e2m1")
    xop = pack_weight(n((F, Z)) / ff[:, None], "e5m2")
    w2p = pack_weight(n((F, R)) * 1 / np.sqrt(F) * ff[:, None] * fr, "e2m1")
    wbp = pack_weight(n((R, N)) * 1 / np.sqrt(R) / fr[:, None], "e2m1")
    return {
        "xf": (n((K, T))).astype(np.float32),
        "ow": (n((K, J)) * 0.7).astype(np.float32),
        "fk": (np.random.uniform(0.5, 2.0, (K, 1)) / fk[:, None]).astype(np.float32),
        "w_words": wp[0],
        "w_scales": wp[1],
        "xo_words": xop[0],
        "xo_scales": xop[1],
        "w2_words": w2p[0],
        "w2_scales": w2p[1],
        "wb_words": wbp[0],
        "wb_scales": wbp[1],
        "rs": (1.0 * n((J, N))).astype(np.float32),
        "offs": striped(idx),
        "offs2": striped(idx2),
    }


def reference(xf, ow, fk, w_words, w_scales, xo_words, xo_scales, w2_words, w2_scales, wb_words, wb_scales, rs, offs, offs2):
    idx = unstriped(offs)
    idx2 = unstriped(offs2)
    wu = unpack_weight(w_words, w_scales, "e2m1")
    xou = unpack_weight(xo_words, xo_scales, "e5m2")
    w2u = unpack_weight(w2_words, w2_scales, "e2m1")
    wbu = unpack_weight(wb_words, wb_scales, "e2m1")
    u = (f64(xf)[:, idx] - f64(ow)) * f64(fk)
    uq = mxq(u, 0, "e4m3")
    xoidx2g = xou[:, idx2]
    a = wu.T @ uq + w2u.T @ xoidx2g
    ha = np.maximum(a, 0.0)
    h1 = np.pad(ha, ((0, 0), (2, 0)))[:, :J]
    hid = ha - 0.5 * h1
    hidq = mxq(hid, 0, "e5m2")
    p = hidq.T @ wbu
    pk2 = np.max(np.abs(p), axis=1, keepdims=True)
    y = p / (pk2 + 0.2) + 0.3 * f64(rs)
    return y

@@ -1,0 +1,208 @@
+from contextlib import ExitStack
+
+import concourse.mybir as mybir
+
+K, T, J, R, F, Z, N = 512, 512, 256, 512, 512, 1024, 256
+FLOPS = 2 * K * R * J + 2 * F * R * J + 2 * R * J * N
+
+F32 = mybir.dt.float32
+BF16 = mybir.dt.bfloat16
+I32 = mybir.dt.int32
+U32 = mybir.dt.uint32
+U16 = mybir.dt.uint16
+U8 = mybir.dt.uint8
+E4M3X4 = mybir.dt.float8_e4m3fn_x4
+E5M2X4 = mybir.dt.float8_e5m2_x4
+E2M1X4 = mybir.dt.float4_e2m1fn_x4
+ALU = mybir.AluOpType
+ACT = mybir.ActivationFunctionType
+
+P = 128
+PACK = 4
+HALF = 128
+HALVES = J // HALF
+LAG = 2
+
+
+def load_scale_rows(queue, plane, scales):
+    for r in range(4):
+        queue.dma_start(out=plane[r:P:32, :].bitcast(I32), in_=scales[0, r:16:4, :].bitcast(I32))
+
+
+def tile_list_sum_offsetpicks_othertable_lagged_rowpeaks_kernel(
+    tc, xf, ow, fk, w_words, w_scales, xo_words, xo_scales, w2_words, w2_scales, wb_words, wb_scales, rs, offs, offs2, out
+):
+    nc = tc.nc
+    with ExitStack() as ctx:
+        held = ctx.enter_context(tc.tile_pool(name="held", bufs=1))
+        psum = ctx.enter_context(tc.psum_pool(name="psum", bufs=1))
+
+        def tile(shape, dtype, name):
+            return held.tile(shape, dtype, name=name, align_bytes=64)
+
+        offs_t = held.tile([P, J // 16], U16, name="offs_t")
+        offs2_t = held.tile([P, J // 16], U16, name="offs2_t")
+        xf_t = [tile([P, T], F32, "xf%d" % i) for i in range(PACK)]
+        ow_t = [tile([P, PACK, HALF], F32, "ow%d" % h) for h in range(HALVES)]
+        fk_t = tile([P, PACK], F32, "fk_t")
+        w_raw = tile([P, 2 * R], U8, "w_raw")
+        w2_raw = tile([P, 2 * R], U8, "w2_raw")
+        ws_raw = tile([P, 2 * R], U8, "ws_raw")
+        xow_t = tile([P, Z], U32, "xow_t")
+        xos_t = tile([P, Z], U8, "xos_t")
+        wb_t = tile([P, 2 * N], U8, "wb_t")
+        wbs_t = tile([P, N], U8, "wbs_t")
+        rs_t = tile([P, HALVES, N], F32, "rs_t")
+        ha = tile([P, PACK * (LAG + J)], F32, "ha")
+
+        nc.vector.memset(ws_raw[:].bitcast(I32), 0)
+        nc.vector.memset(xos_t[:].bitcast(I32), 0)
+        nc.vector.memset(wbs_t[:].bitcast(I32), 0)
+        nc.vector.memset(ha[:, 0 : PACK * LAG], 0.0)
+
+        xf_v = xf.rearrange("(p i) t -> p i t", i=PACK)
+        ow_v = ow.rearrange("(p i) j -> p i j", i=PACK)
+        nc.sync.dma_start(offs_t[:], offs)
+        nc.sync.dma_start(out=xf_t[0][:], in_=xf_v[:, 0, :])
+        nc.sync.dma_start(out=ow_t[0][:], in_=ow_v[:, :, 0:HALF])
+        load_scale_rows(nc.scalar, ws_raw[:, 0:R], w_scales)
+        load_scale_rows(nc.scalar, ws_raw[:, R : 2 * R], w2_scales)
+        load_scale_rows(nc.scalar, xos_t[:], xo_scales)
+        load_scale_rows(nc.gpsimd, wbs_t[:], wb_scales)
+        nc.sync.dma_start(out=xf_t[1][:], in_=xf_v[:, 1, :])
+        nc.sync.dma_start(out=fk_t[:], in_=fk.rearrange("(p i) o -> p (i o)", i=PACK))
+        nc.sync.dma_start(out=xf_t[2][:], in_=xf_v[:, 2, :])
+        nc.sync.dma_start(out=xf_t[3][:], in_=xf_v[:, 3, :])
+        nc.sync.dma_start(offs2_t[:], offs2)
+        nc.sync.dma_start(out=w_raw[:].bitcast(I32), in_=w_words[0].bitcast(I32))
+        nc.sync.dma_start(out=ow_t[1][:], in_=ow_v[:, :, HALF:J])
+        nc.sync.dma_start(out=w2_raw[:].bitcast(I32), in_=w2_words[0].bitcast(I32))
+        nc.sync.dma_start(out=xow_t[:].bitcast(I32), in_=xo_words[0].rearrange("p c b -> p (c b)").bitcast(I32))
+        nc.sync.dma_start(out=wb_t[:].bitcast(I32), in_=wb_words[0].bitcast(I32))
+        nc.sync.dma_start(out=rs_t[:], in_=rs.rearrange("(h p) n -> p h n", p=P))
+
+        ws_t = tile([P, 2 * R], U8, "ws_t")
+        w_t = tile([P, 2 * R], U8, "w_t")
+        w2_t = tile([P, 2 * R], U8, "w2_t")
+        xos_g = tile([P, J], U8, "xos_g")
+        xow_g = tile([P, J], U32, "xow_g")
+        rs3 = tile([P, HALVES, N], F32, "rs3")
+
+        def deal_words(dealt, raw):
+            nc.scalar.copy(
+                out=dealt[:].bitcast(U16).rearrange("p (t b m) -> p b t m", t=PACK, m=8),
+                in_=raw[:].bitcast(U16).rearrange("p (b m t) -> p b t m", t=PACK, m=8),
+            )
+
+        def cols(h):
+            return slice(h * HALF // 16, (h + 1) * HALF // 16)
+
+        diff = [[tile([P, HALF], F32, "diff%d_%d" % (h, i)) for i in range(PACK)] for h in range(HALVES)]
+        u_planes = [tile([P, PACK, HALF], BF16, "u_planes%d" % h) for h in range(HALVES)]
+        u_bf = [tile([P, HALF * PACK], BF16, "u_bf%d" % h) for h in range(HALVES)]
+        u_codes = [tile([P, HALF], U32, "u_codes%d" % h) for h in range(HALVES)]
+        u_scales = [tile([P, HALF], U8, "u_scales%d" % h) for h in range(HALVES)]
+        a_ps = [psum.tile([P, PACK, HALF], F32, name="a_ps%d" % h) for h in range(HALVES)]
+        p_ps = [psum.tile([P, N], F32, name="p_ps%d" % h) for h in range(HALVES)]
+
+        def pick_plane(h, i):
+            nc.vector.tensor_tensor(
+                out=diff[h][i][:], in0=xf_t[i][:].indirect(offs_t[:, cols(h)]), in1=ow_t[h][:, i, :], op=ALU.subtract
+            )
+            nc.scalar.activation(out=u_planes[h][:, i, :], in_=diff[h][i][:], func=ACT.Copy, scale=fk_t[:, i : i + 1])
+
+        def weave(h):
+            nc.vector.tensor_copy(
+                out=u_bf[h][:].rearrange("p (c e i) -> p c i e", e=4, i=PACK),
+                in_=u_planes[h][:].rearrange("p i (c e) -> p c i e", e=4),
+            )
+
+        def quantize_u(h):
+            nc.vector.quantize_mx(out=u_codes[h][:].bitcast(E4M3X4), scales=u_scales[h][:], in_=u_bf[h][:])
+
+        def u_passes(h):
+            for t in range(PACK):
+                nc.tensor.matmul_mx(
+                    out=a_ps[h][:, t, :],
+                    lhsT=w_t[:, 2 * P * t : 2 * P * (t + 1)].bitcast(E2M1X4),
+                    lhsT_scale=ws_t[:, P * t : P * (t + 1)],
+                    rhs=u_codes[h][:].bitcast(E4M3X4),
+                    rhs_scale=u_scales[h][:],
+                    start=(t == 0),
+                    stop=False,
+                )
+
+        def xo_passes(h):
+            js = slice(h * HALF, (h + 1) * HALF)
+            for t in range(PACK):
+                nc.tensor.matmul_mx(
+                    out=a_ps[h][:, t, :],
+                    lhsT=w2_t[:, 2 * P * t : 2 * P * (t + 1)].bitcast(E2M1X4),
+                    lhsT_scale=ws_t[:, R + P * t : R + P * (t + 1)],
+                    rhs=xow_g[:, js].bitcast(E5M2X4),
+                    rhs_scale=xos_g[:, js],
+                    start=False,
+                    stop=(t == PACK - 1),
+                )
+
+        nc.vector.tensor_copy(
+            out=ws_t[:].rearrange("p (w t b m) -> p w b t m", w=2, t=PACK, m=16),
+            in_=ws_raw[:].rearrange("p (w b m t) -> p w b t m", w=2, t=PACK, m=16),
+        )
+        for i in range(PACK):
+            pick_plane(0, i)
+        weave(0)
+        deal_words(w_t, w_raw)
+        nc.vector.tensor_copy(out=xos_g[:], in_=xos_t[:].indirect(offs2_t[:]))
+        quantize_u(0)
+        u_passes(0)
+        for i in range(PACK):
+            pick_plane(1, i)
+        deal_words(w2_t, w2_raw)
+        weave(1)
+        quantize_u(1)
+        u_passes(1)
+        for h in range(HALVES):
+            nc.vector.tensor_copy(out=xow_g[:, h * HALF : (h + 1) * HALF], in_=xow_t[:].indirect(offs2_t[:, cols(h)]))
+            xo_passes(h)
+        nc.scalar.activation(out=rs3[:], in_=rs_t[:], func=ACT.Copy, scale=0.3)
+
+        hid_bf = [tile([P, HALF * PACK], BF16, "hid_bf%d" % h) for h in range(HALVES)]
+        hid_codes = [tile([P, HALF], U32, "hid_codes%d" % h) for h in range(HALVES)]
+        hid_scales = [tile([P, HALF], U8, "hid_scales%d" % h) for h in range(HALVES)]
+        mag = [tile([P, N], F32, "mag%d" % h) for h in range(HALVES)]
+        lifted = [tile([P, N], F32, "lifted%d" % h) for h in range(HALVES)]
+        peak = [tile([P, 1], F32, "peak%d" % h) for h in range(HALVES)]
+        inv = [tile([P, 1], F32, "inv%d" % h) for h in range(HALVES)]
+        res = [tile([P, N], F32, "res%d" % h) for h in range(HALVES)]
+        width = PACK * HALF
+        pad = PACK * LAG
+
+        for h in range(HALVES):
+            now = ha[:, pad + h * width : pad + (h + 1) * width]
+            nc.scalar.activation(
+                out=now.rearrange("p (j t) -> p j t", t=PACK), in_=a_ps[h][:].rearrange("p t j -> p j t"), func=ACT.Relu
+            )
+            nc.vector.scalar_tensor_tensor(
+                out=hid_bf[h][:], in0=ha[:, h * width : (h + 1) * width], scalar=-0.5, in1=now, op0=ALU.mult, op1=ALU.add
+            )
+            nc.vector.quantize_mx(out=hid_codes[h][:].bitcast(E5M2X4), scales=hid_scales[h][:], in_=hid_bf[h][:])
+            nc.tensor.matmul_mx(
+                out=p_ps[h][:],
+                lhsT=hid_codes[h][:].bitcast(E5M2X4),
+                lhsT_scale=hid_scales[h][:],
+                rhs=wb_t[:].bitcast(E2M1X4),
+                rhs_scale=wbs_t[:],
+                start=True,
+                stop=True,
+            )
+        for h in range(HALVES):
+            nc.scalar.activation(out=mag[h][:], in_=p_ps[h][:], func=ACT.Abs)
+            nc.vector.tensor_scalar(
+                out=lifted[h][:], in0=mag[h][:], scalar1=0.2, scalar2=None, op0=ALU.add, op1=ALU.max, accum_out=peak[h][:]
+            )
+            nc.vector.reciprocal(out=inv[h][:], in_=peak[h][:])
+            nc.vector.scalar_tensor_tensor(
+                out=res[h][:], in0=p_ps[h][:], scalar=inv[h][:], in1=rs3[:, h, :], op0=ALU.mult, op1=ALU.add
+            )
+            nc.sync.dma_start(out=out[h * HALF : (h + 1) * HALF, :], in_=res[h][:])

@@ -37,56 +37,52 @@ def tile_list_sum_offsetpicks_othertable_lagged_rowpeaks_kernel(
         held = ctx.enter_context(tc.tile_pool(name="held", bufs=1))
         psum = ctx.enter_context(tc.psum_pool(name="psum", bufs=1))
 
-        def tile(shape, dtype, name):
-            return held.tile(shape, dtype, name=name, align_bytes=64)
+        def tile(shape, dtype, name, tag=None):
+            return held.tile(shape, dtype, name=name, tag=tag or name, align_bytes=64)
 
         offs_t = held.tile([P, J // 16], U16, name="offs_t")
         offs2_t = held.tile([P, J // 16], U16, name="offs2_t")
         xf_t = [tile([P, T], F32, "xf%d" % i) for i in range(PACK)]
-        ow_t = [tile([P, PACK, HALF], F32, "ow%d" % h) for h in range(HALVES)]
+        ow_t = tile([P, PACK * J], F32, "ow_t")
         fk_t = tile([P, PACK], F32, "fk_t")
         w_raw = tile([P, 2 * R], U8, "w_raw")
         w2_raw = tile([P, 2 * R], U8, "w2_raw")
         ws_raw = tile([P, 2 * R], U8, "ws_raw")
         xow_t = tile([P, Z], U32, "xow_t")
         xos_t = tile([P, Z], U8, "xos_t")
-        wb_t = tile([P, 2 * N], U8, "wb_t")
-        wbs_t = tile([P, N], U8, "wbs_t")
-        rs_t = tile([P, HALVES, N], F32, "rs_t")
         ha = tile([P, PACK * (LAG + J)], F32, "ha")
+        xo_at, width_all = 2 * R, 2 * R + J
+        wbs_t = tile([P, N], U8, "wbs_t")
+        rows = tile([P, width_all], U8, "rows")
+        planes = tile([P, width_all], U8, "planes")
 
-        nc.vector.memset(ws_raw[:].bitcast(I32), 0)
         nc.vector.memset(xos_t[:].bitcast(I32), 0)
+        nc.vector.memset(ws_raw[:].bitcast(I32), 0)
         nc.vector.memset(wbs_t[:].bitcast(I32), 0)
+        nc.vector.memset(planes[:].bitcast(I32), 0)
         nc.vector.memset(ha[:, 0 : PACK * LAG], 0.0)
 
         xf_v = xf.rearrange("(p i) t -> p i t", i=PACK)
-        ow_v = ow.rearrange("(p i) j -> p i j", i=PACK)
         nc.sync.dma_start(offs_t[:], offs)
-        nc.sync.dma_start(out=xf_t[0][:], in_=xf_v[:, 0, :])
-        nc.sync.dma_start(out=ow_t[0][:], in_=ow_v[:, :, 0:HALF])
-        load_scale_rows(nc.scalar, ws_raw[:, 0:R], w_scales)
-        load_scale_rows(nc.scalar, ws_raw[:, R : 2 * R], w2_scales)
-        load_scale_rows(nc.scalar, xos_t[:], xo_scales)
+        nc.scalar.dma_start(out=xf_t[0][:], in_=xf_v[:, 0, :])
+        nc.sync.dma_start(offs2_t[:], offs2)
+        nc.scalar.dma_start(out=ow_t[:], in_=ow.rearrange("(p i) j -> p (i j)", i=PACK))
+        nc.sync.dma_start(out=fk_t[:], in_=fk.rearrange("(p i) o -> p (i o)", i=PACK))
+        nc.sync.dma_start(out=xos_t[0:16, :].bitcast(I32), in_=xo_scales[0].bitcast(I32))
+        nc.sync.dma_start(out=ws_raw[0:16, 0:R].bitcast(I32), in_=w_scales[0].bitcast(I32))
+        nc.sync.dma_start(out=ws_raw[0:16, R : 2 * R].bitcast(I32), in_=w2_scales[0].bitcast(I32))
         load_scale_rows(nc.gpsimd, wbs_t[:], wb_scales)
         nc.sync.dma_start(out=xf_t[1][:], in_=xf_v[:, 1, :])
-        nc.sync.dma_start(out=fk_t[:], in_=fk.rearrange("(p i) o -> p (i o)", i=PACK))
         nc.sync.dma_start(out=xf_t[2][:], in_=xf_v[:, 2, :])
         nc.sync.dma_start(out=xf_t[3][:], in_=xf_v[:, 3, :])
-        nc.sync.dma_start(offs2_t[:], offs2)
         nc.sync.dma_start(out=w_raw[:].bitcast(I32), in_=w_words[0].bitcast(I32))
-        nc.sync.dma_start(out=ow_t[1][:], in_=ow_v[:, :, HALF:J])
         nc.sync.dma_start(out=w2_raw[:].bitcast(I32), in_=w2_words[0].bitcast(I32))
         nc.sync.dma_start(out=xow_t[:].bitcast(I32), in_=xo_words[0].rearrange("p c b -> p (c b)").bitcast(I32))
-        nc.sync.dma_start(out=wb_t[:].bitcast(I32), in_=wb_words[0].bitcast(I32))
-        nc.sync.dma_start(out=rs_t[:], in_=rs.rearrange("(h p) n -> p h n", p=P))
 
-        ws_t = tile([P, 2 * R], U8, "ws_t")
         w_t = tile([P, 2 * R], U8, "w_t")
         w2_t = tile([P, 2 * R], U8, "w2_t")
         xos_g = tile([P, J], U8, "xos_g")
         xow_g = tile([P, J], U32, "xow_g")
-        rs3 = tile([P, HALVES, N], F32, "rs3")
 
         def deal_words(dealt, raw):
             nc.scalar.copy(
@@ -97,24 +93,22 @@ def tile_list_sum_offsetpicks_othertable_lagged_rowpeaks_kernel(
         def cols(h):
             return slice(h * HALF // 16, (h + 1) * HALF // 16)
 
-        diff = [[tile([P, HALF], F32, "diff%d_%d" % (h, i)) for i in range(PACK)] for h in range(HALVES)]
-        u_planes = [tile([P, PACK, HALF], BF16, "u_planes%d" % h) for h in range(HALVES)]
+        picked = tile([P, J], F32, "picked")
+        diff = [tile([P, J], F32, "diff%d" % i) for i in range(PACK)]
+        u_all = tile([P, PACK * J], BF16, "u_all")
         u_bf = [tile([P, HALF * PACK], BF16, "u_bf%d" % h) for h in range(HALVES)]
         u_codes = [tile([P, HALF], U32, "u_codes%d" % h) for h in range(HALVES)]
         u_scales = [tile([P, HALF], U8, "u_scales%d" % h) for h in range(HALVES)]
         a_ps = [psum.tile([P, PACK, HALF], F32, name="a_ps%d" % h) for h in range(HALVES)]
         p_ps = [psum.tile([P, N], F32, name="p_ps%d" % h) for h in range(HALVES)]
 
-        def pick_plane(h, i):
-            nc.vector.tensor_tensor(
-                out=diff[h][i][:], in0=xf_t[i][:].indirect(offs_t[:, cols(h)]), in1=ow_t[h][:, i, :], op=ALU.subtract
-            )
-            nc.scalar.activation(out=u_planes[h][:, i, :], in_=diff[h][i][:], func=ACT.Copy, scale=fk_t[:, i : i + 1])
+        def scale_plane(i):
+            nc.scalar.activation(out=u_all[:, i * J : (i + 1) * J], in_=diff[i][:], func=ACT.Copy, scale=fk_t[:, i : i + 1])
 
         def weave(h):
             nc.vector.tensor_copy(
                 out=u_bf[h][:].rearrange("p (c e i) -> p c i e", e=4, i=PACK),
-                in_=u_planes[h][:].rearrange("p i (c e) -> p c i e", e=4),
+                in_=u_all[:].rearrange("p (i h c e) -> p h c i e", i=PACK, h=HALVES, e=4)[:, h],
             )
 
         def quantize_u(h):
@@ -125,7 +119,7 @@ def tile_list_sum_offsetpicks_othertable_lagged_rowpeaks_kernel(
                 nc.tensor.matmul_mx(
                     out=a_ps[h][:, t, :],
                     lhsT=w_t[:, 2 * P * t : 2 * P * (t + 1)].bitcast(E2M1X4),
-                    lhsT_scale=ws_t[:, P * t : P * (t + 1)],
+                    lhsT_scale=planes[:, P * t : P * (t + 1)],
                     rhs=u_codes[h][:].bitcast(E4M3X4),
                     rhs_scale=u_scales[h][:],
                     start=(t == 0),
@@ -133,38 +127,59 @@ def tile_list_sum_offsetpicks_othertable_lagged_rowpeaks_kernel(
                 )
 
         def xo_passes(h):
-            js = slice(h * HALF, (h + 1) * HALF)
             for t in range(PACK):
                 nc.tensor.matmul_mx(
                     out=a_ps[h][:, t, :],
                     lhsT=w2_t[:, 2 * P * t : 2 * P * (t + 1)].bitcast(E2M1X4),
-                    lhsT_scale=ws_t[:, R + P * t : R + P * (t + 1)],
-                    rhs=xow_g[:, js].bitcast(E5M2X4),
-                    rhs_scale=xos_g[:, js],
+                    lhsT_scale=planes[:, R + P * t : R + P * (t + 1)],
+                    rhs=xow_g[:, h * HALF : (h + 1) * HALF].bitcast(E5M2X4),
+                    rhs_scale=planes[:, xo_at + h * HALF : xo_at + (h + 1) * HALF],
                     start=False,
                     stop=(t == PACK - 1),
                 )
 
         nc.vector.tensor_copy(
-            out=ws_t[:].rearrange("p (w t b m) -> p w b t m", w=2, t=PACK, m=16),
+            out=rows[:, 0:xo_at].rearrange("p (w t b m) -> p w b t m", w=2, t=PACK, m=16),
             in_=ws_raw[:].rearrange("p (w b m t) -> p w b t m", w=2, t=PACK, m=16),
         )
-        for i in range(PACK):
-            pick_plane(0, i)
-        weave(0)
-        deal_words(w_t, w_raw)
         nc.vector.tensor_copy(out=xos_g[:], in_=xos_t[:].indirect(offs2_t[:]))
-        quantize_u(0)
-        u_passes(0)
-        for i in range(PACK):
-            pick_plane(1, i)
-        deal_words(w2_t, w2_raw)
-        weave(1)
-        quantize_u(1)
-        u_passes(1)
+        nc.vector.tensor_copy(out=rows[:, xo_at:width_all].bitcast(I32), in_=xos_g[:].bitcast(I32))
+        nc.scalar.activation(out=picked[:], in_=xf_t[0][:].indirect(offs_t[:]), func=ACT.Copy)
+        for r in range(4):
+            nc.scalar.dma_start(out=planes[r:P:32, :].bitcast(I32), in_=rows[r:16:4, :].bitcast(I32))
+        nc.vector.tensor_tensor(out=diff[0][:], in0=picked[:], in1=ow_t[:, 0:J], op=ALU.subtract)
+        scale_plane(0)
+        for i in (1, 2):
+            nc.vector.tensor_tensor(
+                out=diff[i][:], in0=xf_t[i][:].indirect(offs_t[:]), in1=ow_t[:, i * J : (i + 1) * J], op=ALU.subtract
+            )
+            scale_plane(i)
+        wb_t = tile([P, 2 * N], U8, "wb_t", tag="xf1")
+        rs_t = tile([P, HALVES, N], F32, "rs_t", tag="xf2")
+        nc.sync.dma_start(out=wb_t[:].bitcast(I32), in_=wb_words[0].bitcast(I32))
+        nc.sync.dma_start(out=rs_t[:], in_=rs.rearrange("(h p) n -> p h n", p=P))
         for h in range(HALVES):
+            js = slice(h * HALF, (h + 1) * HALF)
+            at = slice(3 * J + h * HALF, 3 * J + (h + 1) * HALF)
+            nc.vector.tensor_tensor(
+                out=diff[3][:, js], in0=xf_t[3][:].indirect(offs_t[:, cols(h)]), in1=ow_t[:, at], op=ALU.subtract
+            )
+        for h in range(HALVES):
+            js = slice(h * HALF, (h + 1) * HALF)
+            at = slice(3 * J + h * HALF, 3 * J + (h + 1) * HALF)
+            nc.vector.tensor_scalar(
+                out=u_all[:, at], in0=diff[3][:, js], scalar1=fk_t[:, 3:4], scalar2=None, op0=ALU.mult
+            )
+        deal_words(w_t, w_raw)
+        deal_words(w2_t, w2_raw)
+        weave(0)
+        weave(1)
+        for h in range(HALVES):
+            quantize_u(h)
+            u_passes(h)
             nc.vector.tensor_copy(out=xow_g[:, h * HALF : (h + 1) * HALF], in_=xow_t[:].indirect(offs2_t[:, cols(h)]))
             xo_passes(h)
+        rs3 = tile([P, HALVES, N], F32, "rs3", tag="w2_raw")
         nc.scalar.activation(out=rs3[:], in_=rs_t[:], func=ACT.Copy, scale=0.3)
 
         hid_bf = [tile([P, HALF * PACK], BF16, "hid_bf%d" % h) for h in range(HALVES)]

@@ -58,26 +58,28 @@ def tile_list_sum_offsetpicks_othertable_lagged_rowpeaks_kernel(
 
         nc.vector.memset(xos_t[:].bitcast(I32), 0)
         nc.vector.memset(ws_raw[:].bitcast(I32), 0)
+        lead = tile([P, PACK * LAG], F32, "lead")
+        nc.vector.memset(lead[:], 0.0)
         nc.vector.memset(wbs_t[:].bitcast(I32), 0)
         nc.vector.memset(planes[:].bitcast(I32), 0)
-        nc.vector.memset(ha[:, 0 : PACK * LAG], 0.0)
 
         xf_v = xf.rearrange("(p i) t -> p i t", i=PACK)
-        nc.sync.dma_start(offs_t[:], offs)
-        nc.scalar.dma_start(out=xf_t[0][:], in_=xf_v[:, 0, :])
         nc.sync.dma_start(offs2_t[:], offs2)
-        nc.scalar.dma_start(out=ow_t[:], in_=ow.rearrange("(p i) j -> p (i j)", i=PACK))
-        nc.sync.dma_start(out=fk_t[:], in_=fk.rearrange("(p i) o -> p (i o)", i=PACK))
+        nc.scalar.dma_start(out=xf_t[0][:], in_=xf_v[:, 0, :])
         nc.sync.dma_start(out=xos_t[0:16, :].bitcast(I32), in_=xo_scales[0].bitcast(I32))
+        nc.scalar.dma_start(out=xf_t[1][:], in_=xf_v[:, 1, :])
+        nc.scalar.activation(out=ha[:, 0 : PACK * LAG], in_=lead[:], func=ACT.Relu)
         nc.sync.dma_start(out=ws_raw[0:16, 0:R].bitcast(I32), in_=w_scales[0].bitcast(I32))
         nc.sync.dma_start(out=ws_raw[0:16, R : 2 * R].bitcast(I32), in_=w2_scales[0].bitcast(I32))
+        nc.sync.dma_start(offs_t[:], offs)
+        nc.sync.dma_start(out=ow_t[:], in_=ow.rearrange("(p i) j -> p (i j)", i=PACK))
+        nc.gpsimd.dma_start(out=fk_t[:], in_=fk.rearrange("(p i) o -> p (i o)", i=PACK))
         load_scale_rows(nc.gpsimd, wbs_t[:], wb_scales)
-        nc.sync.dma_start(out=xf_t[1][:], in_=xf_v[:, 1, :])
         nc.sync.dma_start(out=xf_t[2][:], in_=xf_v[:, 2, :])
         nc.sync.dma_start(out=xf_t[3][:], in_=xf_v[:, 3, :])
-        nc.sync.dma_start(out=w_raw[:].bitcast(I32), in_=w_words[0].bitcast(I32))
-        nc.sync.dma_start(out=w2_raw[:].bitcast(I32), in_=w2_words[0].bitcast(I32))
         nc.sync.dma_start(out=xow_t[:].bitcast(I32), in_=xo_words[0].rearrange("p c b -> p (c b)").bitcast(I32))
+        nc.sync.dma_start(out=w2_raw[:].bitcast(I32), in_=w2_words[0].bitcast(I32))
+        nc.sync.dma_start(out=w_raw[:].bitcast(I32), in_=w_words[0].bitcast(I32))
 
         w_t = tile([P, 2 * R], U8, "w_t")
         w2_t = tile([P, 2 * R], U8, "w2_t")
@@ -93,26 +95,21 @@ def tile_list_sum_offsetpicks_othertable_lagged_rowpeaks_kernel(
         def cols(h):
             return slice(h * HALF // 16, (h + 1) * HALF // 16)
 
-        picked = tile([P, J], F32, "picked")
+        picked = [tile([P, J], F32, "picked%d" % i) for i in range(PACK)]
         diff = [tile([P, J], F32, "diff%d" % i) for i in range(PACK)]
-        u_all = tile([P, PACK * J], BF16, "u_all")
-        u_bf = [tile([P, HALF * PACK], BF16, "u_bf%d" % h) for h in range(HALVES)]
         u_codes = [tile([P, HALF], U32, "u_codes%d" % h) for h in range(HALVES)]
         u_scales = [tile([P, HALF], U8, "u_scales%d" % h) for h in range(HALVES)]
         a_ps = [psum.tile([P, PACK, HALF], F32, name="a_ps%d" % h) for h in range(HALVES)]
         p_ps = [psum.tile([P, N], F32, name="p_ps%d" % h) for h in range(HALVES)]
 
-        def scale_plane(i):
-            nc.scalar.activation(out=u_all[:, i * J : (i + 1) * J], in_=diff[i][:], func=ACT.Copy, scale=fk_t[:, i : i + 1])
-
         def weave(h):
             nc.vector.tensor_copy(
-                out=u_bf[h][:].rearrange("p (c e i) -> p c i e", e=4, i=PACK),
+                out=u_bf[h].rearrange("p (c e i) -> p c i e", e=4, i=PACK),
                 in_=u_all[:].rearrange("p (i h c e) -> p h c i e", i=PACK, h=HALVES, e=4)[:, h],
             )
 
         def quantize_u(h):
-            nc.vector.quantize_mx(out=u_codes[h][:].bitcast(E4M3X4), scales=u_scales[h][:], in_=u_bf[h][:])
+            nc.vector.quantize_mx(out=u_codes[h][:].bitcast(E4M3X4), scales=u_scales[h][:], in_=u_bf[h])
 
         def u_passes(h):
             for t in range(PACK):
@@ -122,8 +119,8 @@ def tile_list_sum_offsetpicks_othertable_lagged_rowpeaks_kernel(
                     lhsT_scale=planes[:, P * t : P * (t + 1)],
                     rhs=u_codes[h][:].bitcast(E4M3X4),
                     rhs_scale=u_scales[h][:],
-                    start=(t == 0),
-                    stop=False,
+                    start=False,
+                    stop=(t == PACK - 1),
                 )
 
         def xo_passes(h):
@@ -134,52 +131,46 @@ def tile_list_sum_offsetpicks_othertable_lagged_rowpeaks_kernel(
                     lhsT_scale=planes[:, R + P * t : R + P * (t + 1)],
                     rhs=xow_g[:, h * HALF : (h + 1) * HALF].bitcast(E5M2X4),
                     rhs_scale=planes[:, xo_at + h * HALF : xo_at + (h + 1) * HALF],
-                    start=False,
-                    stop=(t == PACK - 1),
+                    start=(t == 0),
+                    stop=False,
                 )
 
+        nc.vector.tensor_copy(out=xos_g[:], in_=xos_t[:].indirect(offs2_t[:]))
+        nc.vector.tensor_copy(out=rows[:, xo_at:width_all].bitcast(I32), in_=xos_g[:].bitcast(I32))
         nc.vector.tensor_copy(
             out=rows[:, 0:xo_at].rearrange("p (w t b m) -> p w b t m", w=2, t=PACK, m=16),
             in_=ws_raw[:].rearrange("p (w b m t) -> p w b t m", w=2, t=PACK, m=16),
         )
-        nc.vector.tensor_copy(out=xos_g[:], in_=xos_t[:].indirect(offs2_t[:]))
-        nc.vector.tensor_copy(out=rows[:, xo_at:width_all].bitcast(I32), in_=xos_g[:].bitcast(I32))
-        nc.scalar.activation(out=picked[:], in_=xf_t[0][:].indirect(offs_t[:]), func=ACT.Copy)
         for r in range(4):
-            nc.scalar.dma_start(out=planes[r:P:32, :].bitcast(I32), in_=rows[r:16:4, :].bitcast(I32))
-        nc.vector.tensor_tensor(out=diff[0][:], in0=picked[:], in1=ow_t[:, 0:J], op=ALU.subtract)
-        scale_plane(0)
-        for i in (1, 2):
-            nc.vector.tensor_tensor(
-                out=diff[i][:], in0=xf_t[i][:].indirect(offs_t[:]), in1=ow_t[:, i * J : (i + 1) * J], op=ALU.subtract
-            )
-            scale_plane(i)
-        wb_t = tile([P, 2 * N], U8, "wb_t", tag="xf1")
-        rs_t = tile([P, HALVES, N], F32, "rs_t", tag="xf2")
-        nc.sync.dma_start(out=wb_t[:].bitcast(I32), in_=wb_words[0].bitcast(I32))
+            nc.sync.dma_start(out=planes[r:P:32, :].bitcast(I32), in_=rows[r:16:4, :].bitcast(I32))
+        for i in range(PACK):
+            nc.scalar.activation(out=picked[i][:], in_=xf_t[i][:].indirect(offs_t[:]), func=ACT.Copy)
+        u_all = tile([P, PACK * J], BF16, "u_all", tag="xf3")
+        rs_t = tile([P, HALVES, N], F32, "rs_t", tag="xos_g")
         nc.sync.dma_start(out=rs_t[:], in_=rs.rearrange("(h p) n -> p h n", p=P))
-        for h in range(HALVES):
-            js = slice(h * HALF, (h + 1) * HALF)
-            at = slice(3 * J + h * HALF, 3 * J + (h + 1) * HALF)
-            nc.vector.tensor_tensor(
-                out=diff[3][:, js], in0=xf_t[3][:].indirect(offs_t[:, cols(h)]), in1=ow_t[:, at], op=ALU.subtract
-            )
-        for h in range(HALVES):
-            js = slice(h * HALF, (h + 1) * HALF)
-            at = slice(3 * J + h * HALF, 3 * J + (h + 1) * HALF)
-            nc.vector.tensor_scalar(
-                out=u_all[:, at], in0=diff[3][:, js], scalar1=fk_t[:, 3:4], scalar2=None, op0=ALU.mult
-            )
-        deal_words(w_t, w_raw)
+        wb_t = tile([P, 2 * N], U8, "wb_t", tag="xf2")
+        nc.sync.dma_start(out=wb_t[:].bitcast(I32), in_=wb_words[0].bitcast(I32))
+        for i in range(PACK):
+            nc.vector.tensor_tensor(out=diff[i][:], in0=picked[i][:], in1=ow_t[:, i * J : (i + 1) * J], op=ALU.subtract)
+        for i in range(PACK):
+            plane = u_all[:, i * J : (i + 1) * J]
+            if i < PACK // 2:
+                nc.scalar.activation(out=plane, in_=diff[i][:], func=ACT.Copy, scale=fk_t[:, i : i + 1])
+            else:
+                nc.vector.tensor_scalar(out=plane, in0=diff[i][:], scalar1=fk_t[:, i : i + 1], scalar2=None, op0=ALU.mult)
         deal_words(w2_t, w2_raw)
+        deal_words(w_t, w_raw)
+        for h in range(HALVES):
+            nc.vector.tensor_copy(out=xow_g[:, h * HALF : (h + 1) * HALF], in_=xow_t[:].indirect(offs2_t[:, cols(h)]))
+            xo_passes(h)
+        u_woven = tile([P, PACK * J], BF16, "u_woven", tag="xow_t")
+        u_bf = [u_woven[:, h * PACK * HALF : (h + 1) * PACK * HALF] for h in range(HALVES)]
         weave(0)
         weave(1)
         for h in range(HALVES):
             quantize_u(h)
             u_passes(h)
-            nc.vector.tensor_copy(out=xow_g[:, h * HALF : (h + 1) * HALF], in_=xow_t[:].indirect(offs2_t[:, cols(h)]))
-            xo_passes(h)
-        rs3 = tile([P, HALVES, N], F32, "rs3", tag="w2_raw")
+        rs3 = tile([P, HALVES, N], F32, "rs3", tag="w_raw")
         nc.scalar.activation(out=rs3[:], in_=rs_t[:], func=ACT.Copy, scale=0.3)
 
         hid_bf = [tile([P, HALF * PACK], BF16, "hid_bf%d" % h) for h in range(HALVES)]
@@ -187,20 +178,30 @@ def tile_list_sum_offsetpicks_othertable_lagged_rowpeaks_kernel(
         hid_scales = [tile([P, HALF], U8, "hid_scales%d" % h) for h in range(HALVES)]
         mag = [tile([P, N], F32, "mag%d" % h) for h in range(HALVES)]
         lifted = [tile([P, N], F32, "lifted%d" % h) for h in range(HALVES)]
-        peak = [tile([P, 1], F32, "peak%d" % h) for h in range(HALVES)]
-        inv = [tile([P, 1], F32, "inv%d" % h) for h in range(HALVES)]
+        peak = tile([P, HALVES], F32, "peak")
+        inv = tile([P, HALVES], F32, "inv")
         res = [tile([P, N], F32, "res%d" % h) for h in range(HALVES)]
         width = PACK * HALF
         pad = PACK * LAG
+        step = width // 2
 
         for h in range(HALVES):
-            now = ha[:, pad + h * width : pad + (h + 1) * width]
-            nc.scalar.activation(
-                out=now.rearrange("p (j t) -> p j t", t=PACK), in_=a_ps[h][:].rearrange("p t j -> p j t"), func=ACT.Relu
-            )
-            nc.vector.scalar_tensor_tensor(
-                out=hid_bf[h][:], in0=ha[:, h * width : (h + 1) * width], scalar=-0.5, in1=now, op0=ALU.mult, op1=ALU.add
-            )
+            for c in range(2):
+                lo = h * width + c * step
+                now = ha[:, pad + lo : pad + lo + step]
+                nc.scalar.activation(
+                    out=now.rearrange("p (j t) -> p j t", t=PACK),
+                    in_=a_ps[h][:].rearrange("p t j -> p j t")[:, c * step // PACK : (c + 1) * step // PACK, :],
+                    func=ACT.Relu,
+                )
+                nc.vector.scalar_tensor_tensor(
+                    out=hid_bf[h][:, c * step : (c + 1) * step],
+                    in0=ha[:, lo : lo + step],
+                    scalar=-0.5,
+                    in1=now,
+                    op0=ALU.mult,
+                    op1=ALU.add,
+                )
             nc.vector.quantize_mx(out=hid_codes[h][:].bitcast(E5M2X4), scales=hid_scales[h][:], in_=hid_bf[h][:])
             nc.tensor.matmul_mx(
                 out=p_ps[h][:],
@@ -214,10 +215,17 @@ def tile_list_sum_offsetpicks_othertable_lagged_rowpeaks_kernel(
         for h in range(HALVES):
             nc.scalar.activation(out=mag[h][:], in_=p_ps[h][:], func=ACT.Abs)
             nc.vector.tensor_scalar(
-                out=lifted[h][:], in0=mag[h][:], scalar1=0.2, scalar2=None, op0=ALU.add, op1=ALU.max, accum_out=peak[h][:]
+                out=lifted[h][:],
+                in0=mag[h][:],
+                scalar1=0.2,
+                scalar2=None,
+                op0=ALU.add,
+                op1=ALU.max,
+                accum_out=peak[:, h : h + 1],
             )
-            nc.vector.reciprocal(out=inv[h][:], in_=peak[h][:])
+        nc.vector.reciprocal(out=inv[:], in_=peak[:])
+        for h in range(HALVES):
             nc.vector.scalar_tensor_tensor(
-                out=res[h][:], in0=p_ps[h][:], scalar=inv[h][:], in1=rs3[:, h, :], op0=ALU.mult, op1=ALU.add
+                out=res[h][:], in0=p_ps[h][:], scalar=inv[:, h : h + 1], in1=rs3[:, h, :], op0=ALU.mult, op1=ALU.add
             )
             nc.sync.dma_start(out=out[h * HALF : (h + 1) * HALF, :], in_=res[h][:])

@@ -66,19 +66,19 @@ def tile_list_sum_offsetpicks_othertable_lagged_rowpeaks_kernel(
         xf_v = xf.rearrange("(p i) t -> p i t", i=PACK)
         nc.sync.dma_start(offs2_t[:], offs2)
         nc.scalar.dma_start(out=xf_t[0][:], in_=xf_v[:, 0, :])
-        nc.sync.dma_start(out=xos_t[0:16, :].bitcast(I32), in_=xo_scales[0].bitcast(I32))
-        nc.scalar.dma_start(out=xf_t[1][:], in_=xf_v[:, 1, :])
-        nc.scalar.activation(out=ha[:, 0 : PACK * LAG], in_=lead[:], func=ACT.Relu)
-        nc.sync.dma_start(out=ws_raw[0:16, 0:R].bitcast(I32), in_=w_scales[0].bitcast(I32))
-        nc.sync.dma_start(out=ws_raw[0:16, R : 2 * R].bitcast(I32), in_=w2_scales[0].bitcast(I32))
         nc.sync.dma_start(offs_t[:], offs)
+        nc.scalar.dma_start(out=xf_t[1][:], in_=xf_v[:, 1, :])
+        nc.sync.dma_start(out=xos_t[0:16, :].bitcast(I32), in_=xo_scales[0].bitcast(I32))
+        nc.scalar.dma_start(out=ws_raw[0:16, R : 2 * R].bitcast(I32), in_=w2_scales[0].bitcast(I32))
+        nc.sync.dma_start(out=ws_raw[0:16, 0:R].bitcast(I32), in_=w_scales[0].bitcast(I32))
+        nc.scalar.activation(out=ha[:, 0 : PACK * LAG], in_=lead[:], func=ACT.Relu)
         nc.sync.dma_start(out=ow_t[:], in_=ow.rearrange("(p i) j -> p (i j)", i=PACK))
-        nc.gpsimd.dma_start(out=fk_t[:], in_=fk.rearrange("(p i) o -> p (i o)", i=PACK))
         load_scale_rows(nc.gpsimd, wbs_t[:], wb_scales)
         nc.sync.dma_start(out=xf_t[2][:], in_=xf_v[:, 2, :])
+        nc.sync.dma_start(out=fk_t[:], in_=fk.rearrange("(p i) o -> p (i o)", i=PACK))
         nc.sync.dma_start(out=xf_t[3][:], in_=xf_v[:, 3, :])
-        nc.sync.dma_start(out=xow_t[:].bitcast(I32), in_=xo_words[0].rearrange("p c b -> p (c b)").bitcast(I32))
         nc.sync.dma_start(out=w2_raw[:].bitcast(I32), in_=w2_words[0].bitcast(I32))
+        nc.sync.dma_start(out=xow_t[:].bitcast(I32), in_=xo_words[0].rearrange("p c b -> p (c b)").bitcast(I32))
         nc.sync.dma_start(out=w_raw[:].bitcast(I32), in_=w_words[0].bitcast(I32))
 
         w_t = tile([P, 2 * R], U8, "w_t")
@@ -145,19 +145,16 @@ def tile_list_sum_offsetpicks_othertable_lagged_rowpeaks_kernel(
             nc.sync.dma_start(out=planes[r:P:32, :].bitcast(I32), in_=rows[r:16:4, :].bitcast(I32))
         for i in range(PACK):
             nc.scalar.activation(out=picked[i][:], in_=xf_t[i][:].indirect(offs_t[:]), func=ACT.Copy)
-        u_all = tile([P, PACK * J], BF16, "u_all", tag="xf3")
+        u_all = tile([P, PACK * J], BF16, "u_all")
         rs_t = tile([P, HALVES, N], F32, "rs_t", tag="xos_g")
         nc.sync.dma_start(out=rs_t[:], in_=rs.rearrange("(h p) n -> p h n", p=P))
         wb_t = tile([P, 2 * N], U8, "wb_t", tag="xf2")
         nc.sync.dma_start(out=wb_t[:].bitcast(I32), in_=wb_words[0].bitcast(I32))
         for i in range(PACK):
             nc.vector.tensor_tensor(out=diff[i][:], in0=picked[i][:], in1=ow_t[:, i * J : (i + 1) * J], op=ALU.subtract)
-        for i in range(PACK):
-            plane = u_all[:, i * J : (i + 1) * J]
-            if i < PACK // 2:
-                nc.scalar.activation(out=plane, in_=diff[i][:], func=ACT.Copy, scale=fk_t[:, i : i + 1])
-            else:
-                nc.vector.tensor_scalar(out=plane, in0=diff[i][:], scalar1=fk_t[:, i : i + 1], scalar2=None, op0=ALU.mult)
+            nc.vector.tensor_scalar(
+                out=u_all[:, i * J : (i + 1) * J], in0=diff[i][:], scalar1=fk_t[:, i : i + 1], scalar2=None, op0=ALU.mult
+            )
         deal_words(w2_t, w2_raw)
         deal_words(w_t, w_raw)
         for h in range(HALVES):

from contextlib import ExitStack

import concourse.mybir as mybir

K, T, J, R, F, Z, N = 512, 512, 256, 512, 512, 1024, 256
FLOPS = 2 * K * R * J + 2 * F * R * J + 2 * R * J * N

F32 = mybir.dt.float32
BF16 = mybir.dt.bfloat16
I32 = mybir.dt.int32
U32 = mybir.dt.uint32
U16 = mybir.dt.uint16
U8 = mybir.dt.uint8
E4M3X4 = mybir.dt.float8_e4m3fn_x4
E5M2X4 = mybir.dt.float8_e5m2_x4
E2M1X4 = mybir.dt.float4_e2m1fn_x4
ALU = mybir.AluOpType
ACT = mybir.ActivationFunctionType

P = 128
PACK = 4
HALF = 128
HALVES = J // HALF
LAG = 2


def load_scale_rows(queue, plane, scales):
    for r in range(4):
        queue.dma_start(out=plane[r:P:32, :].bitcast(I32), in_=scales[0, r:16:4, :].bitcast(I32))


def tile_list_sum_offsetpicks_othertable_lagged_rowpeaks_kernel(
    tc, xf, ow, fk, w_words, w_scales, xo_words, xo_scales, w2_words, w2_scales, wb_words, wb_scales, rs, offs, offs2, out
):
    nc = tc.nc
    with ExitStack() as ctx:
        held = ctx.enter_context(tc.tile_pool(name="held", bufs=1))
        psum = ctx.enter_context(tc.psum_pool(name="psum", bufs=1))

        def tile(shape, dtype, name, tag=None):
            return held.tile(shape, dtype, name=name, tag=tag or name, align_bytes=64)

        offs_t = held.tile([P, J // 16], U16, name="offs_t")
        offs2_t = held.tile([P, J // 16], U16, name="offs2_t")
        xf_t = [tile([P, T], F32, "xf%d" % i) for i in range(PACK)]
        ow_t = tile([P, PACK * J], F32, "ow_t")
        fk_t = tile([P, PACK], F32, "fk_t")
        w_raw = tile([P, 2 * R], U8, "w_raw")
        w2_raw = tile([P, 2 * R], U8, "w2_raw")
        ws_raw = tile([P, 2 * R], U8, "ws_raw")
        xow_t = tile([P, Z], U32, "xow_t")
        xos_t = tile([P, Z], U8, "xos_t")
        ha = tile([P, PACK * (LAG + J)], F32, "ha")
        xo_at, width_all = 2 * R, 2 * R + J
        wbs_t = tile([P, N], U8, "wbs_t")
        rows = tile([P, width_all], U8, "rows")
        planes = tile([P, width_all], U8, "planes")

        nc.vector.memset(xos_t[:].bitcast(I32), 0)
        nc.vector.memset(ws_raw[:].bitcast(I32), 0)
        lead = tile([P, PACK * LAG], F32, "lead")
        nc.vector.memset(lead[:], 0.0)
        nc.vector.memset(wbs_t[:].bitcast(I32), 0)
        nc.vector.memset(planes[:].bitcast(I32), 0)

        xf_v = xf.rearrange("(p i) t -> p i t", i=PACK)
        nc.sync.dma_start(offs2_t[:], offs2)
        nc.scalar.dma_start(out=xf_t[0][:], in_=xf_v[:, 0, :])
        nc.sync.dma_start(offs_t[:], offs)
        nc.scalar.dma_start(out=xf_t[1][:], in_=xf_v[:, 1, :])
        nc.sync.dma_start(out=xos_t[0:16, :].bitcast(I32), in_=xo_scales[0].bitcast(I32))
        nc.scalar.dma_start(out=ws_raw[0:16, R : 2 * R].bitcast(I32), in_=w2_scales[0].bitcast(I32))
        nc.sync.dma_start(out=ws_raw[0:16, 0:R].bitcast(I32), in_=w_scales[0].bitcast(I32))
        nc.scalar.activation(out=ha[:, 0 : PACK * LAG], in_=lead[:], func=ACT.Relu)
        nc.sync.dma_start(out=ow_t[:], in_=ow.rearrange("(p i) j -> p (i j)", i=PACK))
        load_scale_rows(nc.gpsimd, wbs_t[:], wb_scales)
        nc.sync.dma_start(out=xf_t[2][:], in_=xf_v[:, 2, :])
        nc.sync.dma_start(out=fk_t[:], in_=fk.rearrange("(p i) o -> p (i o)", i=PACK))
        nc.sync.dma_start(out=xf_t[3][:], in_=xf_v[:, 3, :])
        nc.sync.dma_start(out=w2_raw[:].bitcast(I32), in_=w2_words[0].bitcast(I32))
        nc.sync.dma_start(out=xow_t[:].bitcast(I32), in_=xo_words[0].rearrange("p c b -> p (c b)").bitcast(I32))
        nc.sync.dma_start(out=w_raw[:].bitcast(I32), in_=w_words[0].bitcast(I32))

        w_t = tile([P, 2 * R], U8, "w_t")
        w2_t = tile([P, 2 * R], U8, "w2_t")
        xos_g = tile([P, J], U8, "xos_g")
        xow_g = tile([P, J], U32, "xow_g")

        def deal_words(dealt, raw):
            nc.scalar.copy(
                out=dealt[:].bitcast(U16).rearrange("p (t b m) -> p b t m", t=PACK, m=8),
                in_=raw[:].bitcast(U16).rearrange("p (b m t) -> p b t m", t=PACK, m=8),
            )

        def cols(h):
            return slice(h * HALF // 16, (h + 1) * HALF // 16)

        picked = [tile([P, J], F32, "picked%d" % i) for i in range(PACK)]
        diff = [tile([P, J], F32, "diff%d" % i) for i in range(PACK)]
        u_codes = [tile([P, HALF], U32, "u_codes%d" % h) for h in range(HALVES)]
        u_scales = [tile([P, HALF], U8, "u_scales%d" % h) for h in range(HALVES)]
        a_ps = [psum.tile([P, PACK, HALF], F32, name="a_ps%d" % h) for h in range(HALVES)]
        p_ps = [psum.tile([P, N], F32, name="p_ps%d" % h) for h in range(HALVES)]

        def weave(h):
            nc.vector.tensor_copy(
                out=u_bf[h].rearrange("p (c e i) -> p c i e", e=4, i=PACK),
                in_=u_all[:].rearrange("p (i h c e) -> p h c i e", i=PACK, h=HALVES, e=4)[:, h],
            )

        def quantize_u(h):
            nc.vector.quantize_mx(out=u_codes[h][:].bitcast(E4M3X4), scales=u_scales[h][:], in_=u_bf[h])

        def u_passes(h):
            for t in range(PACK):
                nc.tensor.matmul_mx(
                    out=a_ps[h][:, t, :],
                    lhsT=w_t[:, 2 * P * t : 2 * P * (t + 1)].bitcast(E2M1X4),
                    lhsT_scale=planes[:, P * t : P * (t + 1)],
                    rhs=u_codes[h][:].bitcast(E4M3X4),
                    rhs_scale=u_scales[h][:],
                    start=False,
                    stop=(t == PACK - 1),
                )

        def xo_passes(h):
            for t in range(PACK):
                nc.tensor.matmul_mx(
                    out=a_ps[h][:, t, :],
                    lhsT=w2_t[:, 2 * P * t : 2 * P * (t + 1)].bitcast(E2M1X4),
                    lhsT_scale=planes[:, R + P * t : R + P * (t + 1)],
                    rhs=xow_g[:, h * HALF : (h + 1) * HALF].bitcast(E5M2X4),
                    rhs_scale=planes[:, xo_at + h * HALF : xo_at + (h + 1) * HALF],
                    start=(t == 0),
                    stop=False,
                )

        nc.vector.tensor_copy(out=xos_g[:], in_=xos_t[:].indirect(offs2_t[:]))
        nc.vector.tensor_copy(out=rows[:, xo_at:width_all].bitcast(I32), in_=xos_g[:].bitcast(I32))
        nc.vector.tensor_copy(
            out=rows[:, 0:xo_at].rearrange("p (w t b m) -> p w b t m", w=2, t=PACK, m=16),
            in_=ws_raw[:].rearrange("p (w b m t) -> p w b t m", w=2, t=PACK, m=16),
        )
        for r in range(4):
            nc.sync.dma_start(out=planes[r:P:32, :].bitcast(I32), in_=rows[r:16:4, :].bitcast(I32))
        for i in range(PACK):
            nc.scalar.activation(out=picked[i][:], in_=xf_t[i][:].indirect(offs_t[:]), func=ACT.Copy)
        u_all = tile([P, PACK * J], BF16, "u_all")
        rs_t = tile([P, HALVES, N], F32, "rs_t", tag="xos_g")
        nc.sync.dma_start(out=rs_t[:], in_=rs.rearrange("(h p) n -> p h n", p=P))
        wb_t = tile([P, 2 * N], U8, "wb_t", tag="xf2")
        nc.sync.dma_start(out=wb_t[:].bitcast(I32), in_=wb_words[0].bitcast(I32))
        for i in range(PACK):
            nc.vector.tensor_tensor(out=diff[i][:], in0=picked[i][:], in1=ow_t[:, i * J : (i + 1) * J], op=ALU.subtract)
            nc.vector.tensor_scalar(
                out=u_all[:, i * J : (i + 1) * J], in0=diff[i][:], scalar1=fk_t[:, i : i + 1], scalar2=None, op0=ALU.mult
            )
        deal_words(w2_t, w2_raw)
        deal_words(w_t, w_raw)
        for h in range(HALVES):
            nc.vector.tensor_copy(out=xow_g[:, h * HALF : (h + 1) * HALF], in_=xow_t[:].indirect(offs2_t[:, cols(h)]))
            xo_passes(h)
        u_woven = tile([P, PACK * J], BF16, "u_woven", tag="xow_t")
        u_bf = [u_woven[:, h * PACK * HALF : (h + 1) * PACK * HALF] for h in range(HALVES)]
        weave(0)
        weave(1)
        for h in range(HALVES):
            quantize_u(h)
            u_passes(h)
        rs3 = tile([P, HALVES, N], F32, "rs3", tag="w_raw")
        nc.scalar.activation(out=rs3[:], in_=rs_t[:], func=ACT.Copy, scale=0.3)

        hid_bf = [tile([P, HALF * PACK], BF16, "hid_bf%d" % h) for h in range(HALVES)]
        hid_codes = [tile([P, HALF], U32, "hid_codes%d" % h) for h in range(HALVES)]
        hid_scales = [tile([P, HALF], U8, "hid_scales%d" % h) for h in range(HALVES)]
        mag = [tile([P, N], F32, "mag%d" % h) for h in range(HALVES)]
        lifted = [tile([P, N], F32, "lifted%d" % h) for h in range(HALVES)]
        peak = tile([P, HALVES], F32, "peak")
        inv = tile([P, HALVES], F32, "inv")
        res = [tile([P, N], F32, "res%d" % h) for h in range(HALVES)]
        width = PACK * HALF
        pad = PACK * LAG
        step = width // 2

        for h in range(HALVES):
            for c in range(2):
                lo = h * width + c * step
                now = ha[:, pad + lo : pad + lo + step]
                nc.scalar.activation(
                    out=now.rearrange("p (j t) -> p j t", t=PACK),
                    in_=a_ps[h][:].rearrange("p t j -> p j t")[:, c * step // PACK : (c + 1) * step // PACK, :],
                    func=ACT.Relu,
                )
                nc.vector.scalar_tensor_tensor(
                    out=hid_bf[h][:, c * step : (c + 1) * step],
                    in0=ha[:, lo : lo + step],
                    scalar=-0.5,
                    in1=now,
                    op0=ALU.mult,
                    op1=ALU.add,
                )
            nc.vector.quantize_mx(out=hid_codes[h][:].bitcast(E5M2X4), scales=hid_scales[h][:], in_=hid_bf[h][:])
            nc.tensor.matmul_mx(
                out=p_ps[h][:],
                lhsT=hid_codes[h][:].bitcast(E5M2X4),
                lhsT_scale=hid_scales[h][:],
                rhs=wb_t[:].bitcast(E2M1X4),
                rhs_scale=wbs_t[:],
                start=True,
                stop=True,
            )
        for h in range(HALVES):
            nc.scalar.activation(out=mag[h][:], in_=p_ps[h][:], func=ACT.Abs)
            nc.vector.tensor_scalar(
                out=lifted[h][:],
                in0=mag[h][:],
                scalar1=0.2,
                scalar2=None,
                op0=ALU.add,
                op1=ALU.max,
                accum_out=peak[:, h : h + 1],
            )
        nc.vector.reciprocal(out=inv[:], in_=peak[:])
        for h in range(HALVES):
            nc.vector.scalar_tensor_tensor(
                out=res[h][:], in0=p_ps[h][:], scalar=inv[:, h : h + 1], in1=rs3[:, h, :], op0=ALU.mult, op1=ALU.add
            )
            nc.sync.dma_start(out=out[h * HALF : (h + 1) * HALF, :], in_=res[h][:])
